import numpy as np
CORES = [4,5,6,7,0,1,2,3]
N = 8
def setup_inputs(rng):
    return {"x": rng.standard_normal((N, 128 // N, 64), dtype=np.float32)}
def reference(x):
    g = np.concatenate(list(x), axis=0)
    return {"y": np.broadcast_to(g, (N,) + g.shape)}

from concourse.bass import DstId, RemoteDMATransfer

N = 8
ENGINES = 16

SCRATCH = {
    "gather": ("dram", [N, 128, 8], "float32"),
}
SEMAPHORES = ["loaded", "sent", "arrived", "stored"]


def rank_program(g, core, T, topo):
    rank = T.rank_of(core)
    if rank is None:
        return

    mine = T.gather[rank]
    peers = [c for c in T.cores if c != core]

    g.dma_start(mine, T.x[:]).then_inc(T.sem.loaded, 16)
    g.wait_ge(T.sem.loaded, 16)

    dst_ids = []
    for c in peers:
        a = topo.addr(c)
        dst_ids.append(DstId(rid=a[0], pnc=a[1]))
    g.remote_dma_fused(
        [RemoteDMATransfer(
            dst_ids=dst_ids,
            dma_engine_mask=topo.mask(core, peers[0]),
            remote_sem=T.sem.arrived,
            srcs=[mine],
            dsts=[mine for c in peers],
            alu_op=0,
        )],
        local_sem=T.sem.sent,
    )

    g.wait_ge(T.sem.arrived, ENGINES * (N - 1))
    g.dma_start(T.y[:], T.gather[:]).then_inc(T.sem.stored, 16)
    g.wait_ge(T.sem.sent, ENGINES)
    g.wait_ge(T.sem.stored, 16)
